import numpy as np, ml_dtypes
CORES = [23,119,17,113]
N = 4
import mx_ref
BF = ml_dtypes.bfloat16
def entries(a):
    return np.ascontiguousarray(a.T).reshape(-1)
def table(e):
    return np.ascontiguousarray(np.reshape(e, (-1, 16)).T).astype(np.int32)
def cols(t, e):
    v = np.concatenate([t.reshape(128, -1, 4), np.zeros((128, 1, 4), BF)], axis=1)
    return np.ascontiguousarray(v[:, e]).reshape(128, -1)
def f(rng, *shape):
    return mx_ref.flush((rng.standard_normal(shape, dtype=np.float32) * np.exp2(rng.integers(-2, 3, shape[:-1] + (1,)))).astype(BF))
def wide(rng, *shape, cols=0):
    v = rng.standard_normal(shape, dtype=np.float32) * np.exp2(rng.integers(-12, 13, shape)).astype(np.float32)
    if cols: v *= np.repeat(np.exp2(rng.integers(-cols, cols + 1, shape[:-2] + (1, shape[-1] // 4))) * (rng.random(shape[:-2] + (1, shape[-1] // 4)) > 0.0625), 4, axis=-1).astype(np.float32)
    return mx_ref.flush(v.astype(BF))
T, CAPP = 512, 192
def even(n):
    return [T // n + (k < T % n) for k in range(n)]
def counts(rng, h, moves=10 * N * N):
    n = np.array([[h[(d - s) % N] for d in range(N)] for s in range(N)])[rng.permutation(N)][:, rng.permutation(N)]
    top = np.where(n > 0, CAPP, 0)
    for _ in range(moves):
        a, b = rng.permutation(N)[:2]; c, e = rng.permutation(N)[:2]
        k = rng.integers(0, min(n[a, e], n[b, c], top[a, c] - n[a, c], top[b, e] - n[b, e]) + 1)
        n[a, c] += k; n[b, e] += k; n[a, e] -= k; n[b, c] -= k
    return n
def lists(rng, n, back=False):
    a = np.full((N, N, CAPP), -1)
    for s in range(N):
        p = np.arange(T)[::-1] if back else rng.permutation(T)
        for d in range(N):
            k = rng.permutation(CAPP)[:n[s, d]]
            if back: k = np.sort(k)
            a[s, d, k] = p[:n[s, d]]; p = p[n[s, d]:]
    m = []
    for d in range(N):
        k = np.flatnonzero(a[:, d].reshape(-1) >= 0)
        m.append(table(k[::-1] if back else rng.permutation(k)))
    return {"send": np.stack([table(a[s].reshape(-1)) for s in range(N)]), "mine": np.stack(m), "prev": np.stack([m[(r - 1) % N] for r in range(N)])}
def setup_inputs(rng):
    return {"x": f(rng, N, 128, 4 * T), **lists(rng, counts(rng, even(N)))}
def setup_inputs_empty(rng):
    return {**setup_inputs(rng), **lists(rng, counts(rng, even(N - 1) + [0]))}
def setup_inputs_full(rng):
    return {**setup_inputs(rng), **lists(rng, counts(rng, [min(CAPP, max(0, T - k * CAPP)) for k in range(N)], 0))}
def setup_inputs_reversed(rng):
    return {**setup_inputs(rng), **lists(rng, counts(rng, even(N)), back=True)}
def setup_inputs_spread(rng):
    d = setup_inputs(rng); d["x"] = wide(rng, N, 128, 4 * T, cols=8); return d
def check_inputs(d):
    b = []
    v = np.abs(np.asarray(d["x"]).astype(np.float32))
    if not ((v == 0) | ((v >= 2.0 ** -30) & (v <= 2.0 ** 30))).all(): b.append("x")
    for r in range(N):
        c, m = entries(d["send"][r]), entries(d["mine"][r])
        if c.min() < -1 or not np.array_equal(np.sort(c[c >= 0]), np.arange(T)): b.append("send")
        arrived = np.concatenate([entries(d["send"][s])[r * CAPP:(r + 1) * CAPP] for s in range(N)])
        if not np.array_equal(np.sort(m), np.flatnonzero(arrived >= 0)): b.append("mine")
        if not np.array_equal(d["prev"][r], d["mine"][(r - 1) % N]): b.append("prev")
    return b
def reference(x, send, mine, prev):
    K = []
    for r in range(N):
        arrived = np.concatenate([cols(x[s], entries(send[s])[r * CAPP:(r + 1) * CAPP]) for s in range(N)], axis=1)
        K.append(cols(arrived, entries(mine[r])))
    Q = [mx_ref.quantize(t) for t in K]
    y = np.zeros((N, T, 2 * T), np.float32)
    for r in range(N):
        for p in range(T // 128):
            W = mx_ref.quantize(np.ascontiguousarray(K[r][:, 512 * p:512 * p + 512]))
            y[r, 128 * p:128 * p + 128, :T] = mx_ref.matmul(W, Q[r])
            y[r, 128 * p:128 * p + 128, T:] = mx_ref.matmul(W, Q[(r - 1) % N])
    return {"y": y}

@@ -1,0 +1,266 @@
+from concourse.bass import DstId, RemoteDMATransfer, IndirectOffsetOnAxis
+from concourse.mybir import dt, AluOpType, ActivationFunctionType
+
+N, CH, TC = 4, 192, 512
+RUN = 2 * CH
+PAIR = 2 * RUN
+CHAIN = 3 * CH
+FIRST = 128
+EMPTY = 100000
+
+SCRATCH = {
+    "xs": ("sbuf", [128, 4 * TC], "bfloat16"),
+    "h": ("sbuf", [128, 4 * N * CH], "bfloat16"),
+    "sl": ("sbuf", [128, 48], "int32"),
+    "so": ("sbuf", [128, 48], "uint16"),
+    "ml": ("sbuf", [128, 64], "int32"),
+    "pos": ("sbuf", [128, 64], "int32"),
+    "co": ("sbuf", [128, 64], "uint16"),
+    "fo": ("sbuf", [128, 32], "uint16"),
+    "num": ("sbuf", [128, TC], "int32"),
+    "inv": ("sbuf", [128, 128 * 9], "int32"),
+    "idx": ("sbuf", [128, 9], "int32"),
+    "c1": ("sbuf", [128, CHAIN + PAIR], "float8_e4m3fn_x4"),
+    "p1": ("sbuf", [128, CHAIN + PAIR], "uint8"),
+    "c2": ("sbuf", [128, PAIR], "float8_e4m3fn_x4"),
+    "p2": ("sbuf", [128, PAIR], "uint8"),
+}
+for _k in range(1, 6):
+    SCRATCH["a%d" % _k] = ("sbuf", [128, 64], "int32")
+for _k in range(1, 5):
+    SCRATCH["b%d" % _k] = ("sbuf", [128, 32], "int32")
+for _k in range(6):
+    SCRATCH["w%d" % _k] = ("sbuf", [128, 2 * PAIR], "float32")
+    SCRATCH["yb%d" % _k] = ("sbuf", [128, 2 * TC], "float32")
+for _k in range(4):
+    SCRATCH["ps%d" % _k] = ("psum", [128, 1024], "float32")
+
+SEMAPHORES = ["lsem", "xsem", "msem", "gsem", "isem", "numsem", "v", "s", "t", "near", "far1", "far3", "sent", "scat"]
+
+
+def rank_program(g, core, T, topo):
+    r = T.rank_of(core)
+    if r is None:
+        return
+    sem = T.sem
+    COPY = ActivationFunctionType.Copy
+    cnt = {"v": 0, "s": 0, "t": 0}
+
+    def tick(q, ins):
+        ins.then_inc(sem[q], 1)
+        cnt[q] += 1
+        return cnt[q]
+
+    V, S, PE = g.vector, g.scalar, g.tensor
+
+    def rising(s):
+        return s < 2
+
+    def place(s, d):
+        half = 0 if rising(s) else RUN
+        if s % 2 == d % 2:
+            return True, (CHAIN if rising(d) else 0) + half
+        return False, half
+
+    win = CHAIN if rising(r) else 0
+    if rising(r):
+        order = [r, r + 1, r + 2, r + 3]
+        src = {1: 0, 2: CH, 3: 2 * CH}
+        qpos = [0, 2 * CH]
+        own = (0, 4 * CH)
+        parts = [(0, FIRST), (FIRST, RUN)]
+    else:
+        order = [r + 1, r, r + 3, r + 2]
+        src = {1: 5 * CH, 2: 4 * CH, 3: 3 * CH}
+        qpos = [5 * CH, 3 * CH]
+        own = (1, 2 * CH)
+        parts = [(RUN - FIRST, RUN), (0, RUN - FIRST)]
+    order = [d % N for d in order]
+
+    for k in range(4):
+        for q, e in ((g.sync, 2 * k), (S, 2 * k + 1)):
+            q.dma_start(T.sl[16 * e:16 * e + 16, :], T.send[:]).then_inc(sem.lsem, 16)
+    g.sync.dma_start(T.xs[0:64, :], T.x[0:64, :]).then_inc(sem.xsem, 16)
+    S.dma_start(T.xs[64:128, :], T.x[64:128, :]).then_inc(sem.xsem, 16)
+    for e in range(8):
+        g.sync.dma_start(T.ml[16 * e:16 * e + 16, 0:32], T.mine[:]).then_inc(sem.msem, 16)
+    for e in range(7):
+        g.sync.dma_start(T.ml[16 * e:16 * e + 16, 32:64], T.prev[:]).then_inc(sem.msem, 16)
+    g.dma_start(T.ml[112:128, 32:64], T.prev[:]).then_inc(sem.gsem, 16)
+
+    g.iota(T.num[:], [[1, TC]], 0, 0).then_inc(sem.numsem, 1)
+
+    tick("v", V.memset(T.inv[:], EMPTY))
+    V.wait_ge(sem.lsem, 128)
+    v_off, j = {}, 0
+    while j < N:
+        m = 1
+        while j + m < N and order[j + m] == order[j] + m:
+            m += 1
+        n = tick("v", V.tensor_scalar(T.so[:, 12 * j:12 * (j + m)], T.sl[:, 12 * order[j]:12 * (order[j] + m)],
+                                      0, 4, AluOpType.max, AluOpType.mult))
+        for i in range(m):
+            v_off[j + i] = n
+        j += m
+
+    def gathered(t, a, b):
+        return T.h[:, 4 * a + t:4 * b:4], T.xs[:, t:4 * TC].indirect(T.so[:, a // 16:b // 16])
+
+    V.wait_ge(sem.xsem, 32)
+    S.wait_ge(sem.xsem, 32)
+    vq, seen = [], 0
+    for c0, c1 in parts + [(RUN, 2 * RUN)]:
+        n = max(v_off[i // CH] for i in range(c0, c1, 64))
+        if n > seen:
+            V.wait_ge(sem.v, n)
+            S.wait_ge(sem.v, n)
+            seen = n
+        if c0 < RUN:
+            vjobs, sjobs = [(0, c0, c1), (1, c0, c1)], [(2, c0, c1), (3, c0, c1)]
+        else:
+            vjobs = [(0, c0, c1), (1, c0, c0 + CH)]
+            sjobs = [(2, c0, c1), (3, c0, c1), (1, c0 + CH, c1)]
+        for job in vjobs:
+            vg = tick("v", V.tensor_copy(*gathered(*job)))
+        for job in sjobs:
+            sg = tick("s", S.activation(*gathered(*job), COPY))
+        V.wait_ge(sem.v, vg)
+        V.wait_ge(sem.s, sg)
+        a = qpos[0] + c0 if c0 < RUN else qpos[1]
+        vq.append(tick("v", V.quantize_mx(T.c1[:, a:a + c1 - c0], T.p1[:, a:a + c1 - c0], T.h[:, 4 * c0:4 * c1])))
+    hc, a = own
+    vq.append(tick("v", V.quantize_mx(T.c1[:, a:a + CH], T.p1[:, a:a + CH], T.h[:, 4 * CH * hc:4 * CH * (hc + 1)])))
+
+    dsts = {k: T.cores[(r + k) % N] for k in (1, 2, 3)}
+    feng = topo.engines(core, dsts[1])
+    neng = [e for e in topo.engines(core, dsts[2]) if e not in feng]
+    lands = {1: sem.far1, 2: sem.near, 3: sem.far3}
+
+    def transfer(k, es, codes, m=0, n=RUN):
+        rid, pid, _ = topo.addr(dsts[k])
+        same_pair, c = place(r, (r + k) % N)
+        a, c = src[k] + m, c + m
+        if codes:
+            to = T.c1 if same_pair else T.c2
+            i, o = T.c1[:, a:a + n].bitcast(dt.uint8), to[:, c:c + n].bitcast(dt.uint8)
+        else:
+            to = T.p1 if same_pair else T.p2
+            i, o = T.p1[:, a:a + n], to[:, c:c + n]
+        return RemoteDMATransfer(dst_ids=[DstId(rid=rid, pnc=pid)], dma_engine_mask=sum(1 << e for e in es),
+                                 remote_sem=lands[k], src=i, dst=o)
+
+    few = feng[:len(feng) // 2]
+    nf, nn, n1 = len(feng), len(neng), len(few)
+    for i, es in enumerate((few, feng)):
+        c0, c1 = parts[i]
+        g.wait_ge(sem.v, vq[i])
+        g.remote_dma_fused([transfer(1, es, True, c0, c1 - c0)], local_sem=sem.sent)
+    g.remote_dma_fused([transfer(1, feng, False)], local_sem=sem.sent)
+    g.wait_ge(sem.v, vq[2])
+    for codes in (True, False):
+        g.remote_dma_fused([transfer(3, feng, codes), transfer(2, neng, codes)], local_sem=sem.sent)
+    n_far1, n_far3, n_near = n1 + 2 * nf, 2 * nf, 2 * nn
+    n_sent = n_far1 + n_far3 + n_near
+
+    ge, mul, add = AluOpType.is_ge, AluOpType.mult, AluOpType.add
+    V.wait_ge(sem.msem, 240)
+    V.wait_ge(sem.gsem, 16)
+    tick("v", V.tensor_scalar(T.a1[:], T.ml[:], CH, 3 * CH, ge, mul))
+    tick("v", V.tensor_scalar(T.a2[:, 0:32], T.ml[:, 0:32], 2 * CH, -4 * CH, ge, mul))
+    tick("v", V.tensor_scalar(T.a2[:, 32:64], T.ml[:, 32:64], 2 * CH, -2 * CH, ge, mul))
+    n = tick("v", V.tensor_scalar(T.a3[:], T.ml[:], 3 * CH, 3 * CH, ge, mul))
+    V.wait_ge(sem.v, n)
+    tick("v", V.tensor_tensor(T.a4[:], T.ml[:], T.a2[:], add))
+    n = tick("v", V.tensor_tensor(T.a5[:], T.a1[:], T.a3[:], add))
+    V.wait_ge(sem.v, n)
+    n = tick("v", V.tensor_tensor(T.pos[:], T.a4[:], T.a5[:], add))
+    V.wait_ge(sem.v, n)
+    tick("v", V.tensor_scalar(T.b1[:], T.pos[:, 0:32], 127, None, AluOpType.bitwise_and))
+    n = tick("v", V.tensor_scalar(T.b2[:], T.pos[:, 0:32], 7, None, AluOpType.arith_shift_right))
+    v_co = tick("v", V.tensor_copy(T.co[:], T.pos[:]))
+    V.wait_ge(sem.v, n)
+    n = tick("v", V.tensor_scalar(T.b3[:], T.b1[:], 9, None, mul))
+    V.wait_ge(sem.v, n)
+    n = tick("v", V.tensor_tensor(T.b4[:], T.b3[:], T.b2[:], add))
+    V.wait_ge(sem.v, n)
+    n = tick("v", V.tensor_copy(T.fo[:], T.b4[:]))
+    V.wait_ge(sem.numsem, 1)
+    V.wait_ge(sem.v, n)
+    v_inv = tick("v", V.tensor_copy(T.inv[:, 0:1152].indirect(T.fo[:, 0:32]), T.num[:]))
+    g.sync.wait_ge(sem.v, v_inv)
+    g.sync.dma_start(T.idx[:], T.inv[0:1, :]).then_inc(sem.isem, 16)
+
+    PS = [T["ps%d" % u] for u in range(4)]
+    me = r % 2
+    blocks = [3 * me + i for i in range(3)] + [3 * (1 - me) + i for i in range(3)]
+    W = [T["w%d" % b] for b in blocks]
+    Y = [T["yb%d" % b] for b in blocks]
+    icol = [6 * (b // 3) + b % 3 for b in blocks]
+    NC, FC = PAIR * me, PAIR * (1 - me)
+    A0 = 0 if rising((r - 1) % N) else RUN
+    B0 = RUN - A0
+
+    def near(a, b):
+        return T.c1[:, win + a:win + b], T.p1[:, win + a:win + b]
+
+    def far(a, b):
+        return T.c2[:, a:b], T.p2[:, a:b]
+
+    def product(j, side, u, bank, a, b):
+        st = (near if j < 3 else far)(CH + 128 * (j % 3), CH + 128 * (j % 3) + 128)
+        mv = side(a, b)
+        return tick("t", PE.matmul_mx(PS[u][:, 512 * bank:512 * bank + b - a], st[0], st[1], mv[0], mv[1], True, True))
+
+    v_ga, s_ga = {}, {}
+    readers = {}
+
+    def free(u):
+        for q, n in readers.get(u, ()):
+            PE.wait_ge(sem[q], n)
+
+    def half(j, side, u):
+        free(u)
+        product(j, side, u, 0, 0, 512)
+        return product(j, side, u, 1, 512, PAIR)
+
+    def by_scalar(j, u, bank, w, n, t):
+        S.wait_ge(sem.t, t)
+        return tick("s", S.activation(W[j][:, w:w + n], PS[u][:, 512 * bank:512 * bank + n], COPY))
+
+    def by_vector(j, u, bank, w, n, t):
+        V.wait_ge(sem.t, t)
+        return tick("v", V.tensor_copy(W[j][:, w:w + n], PS[u][:, 512 * bank:512 * bank + n]))
+
+    def columns(j, vn, sn):
+        for q in (V, S):
+            q.wait_ge(sem.v, max(vn, v_co))
+            q.wait_ge(sem.s, sn)
+        s_ga[j] = tick("s", S.activation(Y[j][:, 0:TC], W[j][:, CH:2 * PAIR].indirect(T.co[:, 0:32]), COPY))
+        v_ga[j] = tick("v", V.tensor_copy(Y[j][:, TC:2 * TC], W[j][:, 0:2 * PAIR].indirect(T.co[:, 32:64])))
+
+    PE.wait_ge(sem.v, vq[3])
+    PE.wait_ge(sem.near, n_near)
+    readers[0] = (("s", by_scalar(0, 0, 0, NC, PAIR, half(0, near, 0))),)
+    PE.wait_ge(sem.far1, n_far1)
+    readers[2] = (("v", by_vector(0, 2, 0, FC + A0, RUN, product(0, far, 2, 0, A0, A0 + RUN))),)
+    PE.wait_ge(sem.far3, n_far3)
+    vn = by_vector(0, 3, 0, FC + B0, CH, product(0, far, 3, 0, B0, B0 + CH))
+    sn = by_scalar(0, 3, 1, FC + B0 + CH, CH, product(0, far, 3, 1, B0 + CH, B0 + RUN))
+    readers[3] = (("v", vn), ("s", sn))
+    columns(0, vn, sn)
+    for j in range(1, 6):
+        u = 2 * (1 - j % 2)
+        sn = by_scalar(j, u, 0, NC, PAIR, half(j, near, u))
+        readers[u] = (("s", sn),)
+        vn = by_vector(j, u + 1, 0, FC, PAIR, half(j, far, u + 1))
+        readers[u + 1] = (("v", vn),)
+        columns(j, vn, sn)
+
+    g.wait_ge(sem.isem, 16)
+    for j in range(6):
+        g.wait_ge(sem.v, v_ga[j])
+        g.wait_ge(sem.s, s_ga[j])
+        g.indirect_dma_start(T.y[:], IndirectOffsetOnAxis(ap=T.idx[:, icol[j]:icol[j] + 1], axis=0), Y[j][:], None,
+                             bounds_check=TC - 1, oob_is_err=False).then_inc(sem.scat, 16)
+    g.wait_ge(sem.sent, n_sent)
+    g.wait_ge(sem.scat, 96)

@@ -5,37 +5,54 @@ N, CH, TC = 4, 192, 512
 RUN = 2 * CH
 PAIR = 2 * RUN
 CHAIN = 3 * CH
-FIRST = 128
 EMPTY = 100000
+SHIFT = 96
+BANK = 512
+PAD = 64
+AHEAD = {"o": 0, "a": 1, "n": 2, "b": 3}
 
 SCRATCH = {
     "xs": ("sbuf", [128, 4 * TC], "bfloat16"),
-    "h": ("sbuf", [128, 4 * N * CH], "bfloat16"),
+    "h": ("sbuf", [128, 4 * (N * CH + PAD)], "bfloat16"),
     "sl": ("sbuf", [128, 48], "int32"),
     "so": ("sbuf", [128, 48], "uint16"),
-    "ml": ("sbuf", [128, 64], "int32"),
-    "pos": ("sbuf", [128, 64], "int32"),
-    "co": ("sbuf", [128, 64], "uint16"),
-    "fo": ("sbuf", [128, 32], "uint16"),
-    "num": ("sbuf", [128, TC], "int32"),
-    "inv": ("sbuf", [128, 128 * 9], "int32"),
-    "idx": ("sbuf", [128, 9], "int32"),
+    "ml": ("sbuf", [128, 80], "int32"),
+    "co": ("sbuf", [128, 80], "uint16"),
+    "fo": ("sbuf", [128, 16], "uint16"),
+    "sh": ("sbuf", [128, 1], "float32"),
+    "num": ("sbuf", [128, TC // 2], "float32"),
+    "inv": ("sbuf", [128, SHIFT + PAIR], "float32"),
+    "tr": ("sbuf", [128, 6 * 32], "float32"),
+    "up": ("sbuf", [128, 6], "float32"),
+    "idx": ("sbuf", [128, 6], "int32"),
     "c1": ("sbuf", [128, CHAIN + PAIR], "float8_e4m3fn_x4"),
     "p1": ("sbuf", [128, CHAIN + PAIR], "uint8"),
     "c2": ("sbuf", [128, PAIR], "float8_e4m3fn_x4"),
     "p2": ("sbuf", [128, PAIR], "uint8"),
+    "ps": ("psum", [128, 8 * BANK], "float32"),
 }
-for _k in range(1, 6):
-    SCRATCH["a%d" % _k] = ("sbuf", [128, 64], "int32")
-for _k in range(1, 5):
-    SCRATCH["b%d" % _k] = ("sbuf", [128, 32], "int32")
 for _k in range(6):
     SCRATCH["w%d" % _k] = ("sbuf", [128, 2 * PAIR], "float32")
     SCRATCH["yb%d" % _k] = ("sbuf", [128, 2 * TC], "float32")
-for _k in range(4):
-    SCRATCH["ps%d" % _k] = ("psum", [128, 1024], "float32")
 
-SEMAPHORES = ["lsem", "xsem", "msem", "gsem", "isem", "numsem", "v", "s", "t", "near", "far1", "far3", "sent", "scat"]
+SEMAPHORES = ["lsem", "xsem", "msem", "rsem", "gsem", "numsem", "v", "s", "t", "sent", "scat",
+              "a1", "a2", "b1", "n1"]
+
+PIECES = [(0, 64, 128), (64, 384, 576), (384, 576, 320), (576, 768, 0)]
+LISTS = (3, 4)
+CALLS = [[("b1", "codes", 0, 64)],
+         [("b1", "codes", 64, 384)],
+         [("n1", "codes", 192, 384)],
+         [("b1", "scales", 0, 384)],
+         [("a1", "codes", 384, 576), ("n1", "codes", 384, 576)],
+         [("n1", "scales", 192, 576)],
+         [("a1", "scales", 384, 768)],
+         [("a2", "codes", 576, 768)]]
+PLAN = ([("s", "o", 0), ("s", "b", 0), ("v", "b", 1), ("s", "o", 1), ("s", "n", 0), ("v", "Ra", 0), ("v", "n", 1),
+         ("s", "mine", 0), ("v", "Pa", 0), ("v", "prev0", 0), ("s", "prev1", 0), ("v", "a", 1), ("s", "mine", 1),
+         ("v", "prev", 1)]
+        + [step for j in range(2, 6)
+           for step in (("s", "pair", j), ("v", "other", j), ("s", "mine", j), ("v", "prev", j))])
 
 
 def rank_program(g, core, T, topo):
@@ -53,214 +70,224 @@ def rank_program(g, core, T, topo):
 
     V, S, PE = g.vector, g.scalar, g.tensor
 
-    def rising(s):
-        return s < 2
+    def copy(q, out, in_):
+        return tick(q, V.tensor_copy(out, in_) if q == "v" else S.activation(out, in_, COPY))
 
-    def place(s, d):
-        half = 0 if rising(s) else RUN
-        if s % 2 == d % 2:
-            return True, (CHAIN if rising(d) else 0) + half
-        return False, half
+    def rising(s):
+        return s % 2 == 0
 
     win = CHAIN if rising(r) else 0
-    if rising(r):
-        order = [r, r + 1, r + 2, r + 3]
-        src = {1: 0, 2: CH, 3: 2 * CH}
-        qpos = [0, 2 * CH]
-        own = (0, 4 * CH)
-        parts = [(0, FIRST), (FIRST, RUN)]
-    else:
-        order = [r + 1, r, r + 3, r + 2]
-        src = {1: 5 * CH, 2: 4 * CH, 3: 3 * CH}
-        qpos = [5 * CH, 3 * CH]
-        own = (1, 2 * CH)
-        parts = [(RUN - FIRST, RUN), (0, RUN - FIRST)]
-    order = [d % N for d in order]
+    base = 0 if rising(r) else CHAIN
+    order = [(r + k) % N for k in (range(N) if rising(r) else reversed(range(N)))]
 
-    for k in range(4):
-        for q, e in ((g.sync, 2 * k), (S, 2 * k + 1)):
-            q.dma_start(T.sl[16 * e:16 * e + 16, :], T.send[:]).then_inc(sem.lsem, 16)
-    g.sync.dma_start(T.xs[0:64, :], T.x[0:64, :]).then_inc(sem.xsem, 16)
-    S.dma_start(T.xs[64:128, :], T.x[64:128, :]).then_inc(sem.xsem, 16)
-    for e in range(8):
-        g.sync.dma_start(T.ml[16 * e:16 * e + 16, 0:32], T.mine[:]).then_inc(sem.msem, 16)
-    for e in range(7):
-        g.sync.dma_start(T.ml[16 * e:16 * e + 16, 32:64], T.prev[:]).then_inc(sem.msem, 16)
-    g.dma_start(T.ml[112:128, 32:64], T.prev[:]).then_inc(sem.gsem, 16)
+    def column(s, kind):
+        return {"P": 0, "R": CH}[kind] if rising(s) else {"R": RUN, "P": RUN + CH}[kind]
 
-    g.iota(T.num[:], [[1, TC]], 0, 0).then_inc(sem.numsem, 1)
+    for q, e in ((g.sync, 0), (S, 1)):
+        q.dma_start(T.sl[16 * e:16 * e + 16, :], T.send[:]).then_inc(sem.lsem, 16)
+        q.dma_start(T.xs[64 * e:64 * e + 64, :], T.x[64 * e:64 * e + 64, :]).then_inc(sem.xsem, 16)
+    for e in range(2):
+        rows = slice(16 * e, 16 * e + 16)
+        g.sync.dma_start(T.ml[rows, 0:32], T.mine[:]).then_inc(sem.msem, 16)
+        g.sync.dma_start(T.ml[rows, 32:48], T.mine[:, 16 * e:16 * e + 16]).then_inc(sem.msem, 16)
+    g.sync.dma_start(T.ml[0:16, 48:80], T.prev[:]).then_inc(sem.msem, 16)
+    g.dma_start(T.ml[16:32, 48:80], T.prev[:]).then_inc(sem.gsem, 16)
+    g.sync.wait_ge(sem.msem, 80)
+    g.sync.wait_ge(sem.gsem, 16)
+    for a in range(1, 4):
+        g.sync.dma_start(T.ml[32 * a:32 * a + 32, :], T.ml[0:32, :]).then_inc(sem.rsem, 16)
 
-    tick("v", V.memset(T.inv[:], EMPTY))
-    V.wait_ge(sem.lsem, 128)
-    v_off, j = {}, 0
+    g.iota(T.num[:], [[1, TC // 2]], 0, 0, allow_small_or_imprecise_dtypes=True).then_inc(sem.numsem, 1)
+    for k in range(6):
+        tick("v", V.memset(T.inv[:, SHIFT + 128 * k:SHIFT + 128 * k + 32], float(EMPTY)))
+    for a in range(4):
+        tick("v", V.memset(T.sh[32 * a:32 * a + 32, :], float(SHIFT - 32 * a)))
+    pad = 0 if rising(r) else PAD
+    a = PAIR if rising(r) else 0
+    tick("v", V.memset(T.h[:, 4 * a:4 * (a + PAD)], 0.0))
+    V.wait_ge(sem.lsem, 32)
+    j = 0
     while j < N:
         m = 1
         while j + m < N and order[j + m] == order[j] + m:
             m += 1
-        n = tick("v", V.tensor_scalar(T.so[:, 12 * j:12 * (j + m)], T.sl[:, 12 * order[j]:12 * (order[j] + m)],
+        n = tick("v", V.tensor_scalar(T.so[0:32, 12 * j:12 * (j + m)], T.sl[0:32, 12 * order[j]:12 * (order[j] + m)],
                                       0, 4, AluOpType.max, AluOpType.mult))
-        for i in range(m):
-            v_off[j + i] = n
         j += m
+    V.wait_ge(sem.v, n)
+    for a in range(1, 4):
+        n = copy("v", T.so[32 * a:32 * a + 32, :], T.so[0:32, :])
+
+    add = AluOpType.add
+    made = {}
+
+    def invert():
+        V.wait_ge(sem.rsem, 48)
+        n = tick("v", V.tensor_scalar(T.fo[:], T.ml[:, 32:48], T.sh[:], None, add))
+        made["co"] = copy("v", T.co[:], T.ml[:])
+        V.wait_ge(sem.numsem, 1)
+        V.wait_ge(sem.v, n)
+        made["inv"] = copy("v", T.inv[:].indirect(T.fo[:]), T.num[:])
+
+    def turn():
+        V.wait_ge(sem.v, made["inv"])
+        for k in range(6):
+            a = SHIFT + 128 * k
+            n = tick("v", V.transpose(T.tr[:, 32 * k:32 * k + 32], T.inv[:, a:a + 32]))
+        V.wait_ge(sem.v, n)
+        n = tick("v", V.tensor_scalar(T.up[:], T.tr[:, 16:192:32], TC // 2, None, add))
+        V.wait_ge(sem.v, n)
+        made["idx"] = tick("v", V.tensor_tensor(T.idx[:], T.tr[:, 0:192:32], T.up[:], AluOpType.min))
 
     def gathered(t, a, b):
-        return T.h[:, 4 * a + t:4 * b:4], T.xs[:, t:4 * TC].indirect(T.so[:, a // 16:b // 16])
+        return T.h[:, 4 * (pad + a) + t:4 * (pad + b):4], T.xs[:, t:4 * TC].indirect(T.so[:, a // 16:b // 16])
 
-    V.wait_ge(sem.xsem, 32)
-    S.wait_ge(sem.xsem, 32)
-    vq, seen = [], 0
-    for c0, c1 in parts + [(RUN, 2 * RUN)]:
-        n = max(v_off[i // CH] for i in range(c0, c1, 64))
-        if n > seen:
-            V.wait_ge(sem.v, n)
-            S.wait_ge(sem.v, n)
-            seen = n
-        if c0 < RUN:
-            vjobs, sjobs = [(0, c0, c1), (1, c0, c1)], [(2, c0, c1), (3, c0, c1)]
-        else:
-            vjobs = [(0, c0, c1), (1, c0, c0 + CH)]
-            sjobs = [(2, c0, c1), (3, c0, c1), (1, c0 + CH, c1)]
-        for job in vjobs:
-            vg = tick("v", V.tensor_copy(*gathered(*job)))
-        for job in sjobs:
-            sg = tick("s", S.activation(*gathered(*job), COPY))
-        V.wait_ge(sem.v, vg)
-        V.wait_ge(sem.s, sg)
-        a = qpos[0] + c0 if c0 < RUN else qpos[1]
-        vq.append(tick("v", V.quantize_mx(T.c1[:, a:a + c1 - c0], T.p1[:, a:a + c1 - c0], T.h[:, 4 * c0:4 * c1])))
-    hc, a = own
-    vq.append(tick("v", V.quantize_mx(T.c1[:, a:a + CH], T.p1[:, a:a + CH], T.h[:, 4 * CH * hc:4 * CH * (hc + 1)])))
+    def quantise(a, c0, c1):
+        n = c1 - c0
+        return tick("v", V.quantize_mx(T.c1[:, a:a + n], T.p1[:, a:a + n], T.h[:, 4 * (pad + c0):4 * (pad + c1)]))
+
+    def span(u0, u1):
+        return (PAIR - u1, PAIR - u0) if rising(r) else (u0, u1)
+
+    for q in (V, S):
+        q.wait_ge(sem.v, n)
+        q.wait_ge(sem.xsem, 32)
+    vq = []
+    for i, (u0, u1, share) in enumerate(PIECES):
+        c0, c1 = span(u0, u1)
+        if i == LISTS[0]:
+            invert()
+        if i == LISTS[1]:
+            turn()
+        for t in range(4):
+            c = c0 + min(max(share - t * (c1 - c0), 0), c1 - c0)
+            if c > c0:
+                copy("v", *gathered(t, c0, c))
+            if c < c1:
+                copy("s", *gathered(t, c, c1))
+        if share:
+            V.wait_ge(sem.v, cnt["v"])
+        V.wait_ge(sem.s, cnt["s"])
+        c0, c1 = span(min(u0, u1 - 128), u1)
+        vq.append((u0, u1, quantise(base + c0, c0, c1)))
+    v_own = quantise(win + column(r, "R"), *span(CHAIN, PAIR))
+    if LISTS[0] == len(PIECES):
+        invert()
+    if LISTS[1] == len(PIECES):
+        turn()
+    v_co, v_idx = made["co"], made["idx"]
 
     dsts = {k: T.cores[(r + k) % N] for k in (1, 2, 3)}
     feng = topo.engines(core, dsts[1])
     neng = [e for e in topo.engines(core, dsts[2]) if e not in feng]
-    lands = {1: sem.far1, 2: sem.near, 3: sem.far3}
+    landed = {}
 
-    def transfer(k, es, codes, m=0, n=RUN):
+    def transfer(lands, what, u0, u1):
+        k = AHEAD[lands[0]]
+        d = (r + k) % N
         rid, pid, _ = topo.addr(dsts[k])
-        same_pair, c = place(r, (r + k) % N)
-        a, c = src[k] + m, c + m
-        if codes:
-            to = T.c1 if same_pair else T.c2
-            i, o = T.c1[:, a:a + n].bitcast(dt.uint8), to[:, c:c + n].bitcast(dt.uint8)
+        same = r // 2 == d // 2
+        c0, c1 = span(u0, u1)
+        run = span((3 - k) * CH, (5 - k) * CH)[0]
+        c = ((CHAIN if rising(d) else 0) if same else 0) + (0 if rising(r) else RUN) + c0 - run
+        a, n = base + c0, c1 - c0
+        if what == "scales":
+            i, o = T.p1[:, a:a + n], (T.p1 if same else T.p2)[:, c:c + n]
         else:
-            to = T.p1 if same_pair else T.p2
-            i, o = T.p1[:, a:a + n], to[:, c:c + n]
-        return RemoteDMATransfer(dst_ids=[DstId(rid=rid, pnc=pid)], dma_engine_mask=sum(1 << e for e in es),
-                                 remote_sem=lands[k], src=i, dst=o)
+            i, o = T.c1[:, a:a + n].bitcast(dt.uint8), (T.c1 if same else T.c2)[:, c:c + n].bitcast(dt.uint8)
+        es = neng if k == 2 else feng
+        landed[lands] = landed.get(lands, 0) + len(es)
+        return RemoteDMATransfer(dst_ids=[DstId(rid=rid, pnc=pid)], remote_sem=sem[lands], src=i, dst=o,
+                                 dma_engine_mask=sum(1 << e for e in es))
 
-    few = feng[:len(feng) // 2]
-    nf, nn, n1 = len(feng), len(neng), len(few)
-    for i, es in enumerate((few, feng)):
-        c0, c1 = parts[i]
-        g.wait_ge(sem.v, vq[i])
-        g.remote_dma_fused([transfer(1, es, True, c0, c1 - c0)], local_sem=sem.sent)
-    g.remote_dma_fused([transfer(1, feng, False)], local_sem=sem.sent)
-    g.wait_ge(sem.v, vq[2])
-    for codes in (True, False):
-        g.remote_dma_fused([transfer(3, feng, codes), transfer(2, neng, codes)], local_sem=sem.sent)
-    n_far1, n_far3, n_near = n1 + 2 * nf, 2 * nf, 2 * nn
-    n_sent = n_far1 + n_far3 + n_near
+    seen = 0
+    for call in CALLS:
+        n = max(n for u0, u1, n in vq for job in call if u0 < job[3] and job[2] < u1)
+        if n > seen:
+            g.wait_ge(sem.v, n)
+            seen = n
+        g.remote_dma_fused([transfer(*job) for job in call], local_sem=sem.sent)
+    n_sent = sum(landed.values())
 
-    ge, mul, add = AluOpType.is_ge, AluOpType.mult, AluOpType.add
-    V.wait_ge(sem.msem, 240)
-    V.wait_ge(sem.gsem, 16)
-    tick("v", V.tensor_scalar(T.a1[:], T.ml[:], CH, 3 * CH, ge, mul))
-    tick("v", V.tensor_scalar(T.a2[:, 0:32], T.ml[:, 0:32], 2 * CH, -4 * CH, ge, mul))
-    tick("v", V.tensor_scalar(T.a2[:, 32:64], T.ml[:, 32:64], 2 * CH, -2 * CH, ge, mul))
-    n = tick("v", V.tensor_scalar(T.a3[:], T.ml[:], 3 * CH, 3 * CH, ge, mul))
-    V.wait_ge(sem.v, n)
-    tick("v", V.tensor_tensor(T.a4[:], T.ml[:], T.a2[:], add))
-    n = tick("v", V.tensor_tensor(T.a5[:], T.a1[:], T.a3[:], add))
-    V.wait_ge(sem.v, n)
-    n = tick("v", V.tensor_tensor(T.pos[:], T.a4[:], T.a5[:], add))
-    V.wait_ge(sem.v, n)
-    tick("v", V.tensor_scalar(T.b1[:], T.pos[:, 0:32], 127, None, AluOpType.bitwise_and))
-    n = tick("v", V.tensor_scalar(T.b2[:], T.pos[:, 0:32], 7, None, AluOpType.arith_shift_right))
-    v_co = tick("v", V.tensor_copy(T.co[:], T.pos[:]))
-    V.wait_ge(sem.v, n)
-    n = tick("v", V.tensor_scalar(T.b3[:], T.b1[:], 9, None, mul))
-    V.wait_ge(sem.v, n)
-    n = tick("v", V.tensor_tensor(T.b4[:], T.b3[:], T.b2[:], add))
-    V.wait_ge(sem.v, n)
-    n = tick("v", V.tensor_copy(T.fo[:], T.b4[:]))
-    V.wait_ge(sem.numsem, 1)
-    V.wait_ge(sem.v, n)
-    v_inv = tick("v", V.tensor_copy(T.inv[:, 0:1152].indirect(T.fo[:, 0:32]), T.num[:]))
-    g.sync.wait_ge(sem.v, v_inv)
-    g.sync.dma_start(T.idx[:], T.inv[0:1, :]).then_inc(sem.isem, 16)
+    sender = {c: (r - k) % N for c, k in AHEAD.items()}
 
-    PS = [T["ps%d" % u] for u in range(4)]
-    me = r % 2
-    blocks = [3 * me + i for i in range(3)] + [3 * (1 - me) + i for i in range(3)]
-    W = [T["w%d" % b] for b in blocks]
-    Y = [T["yb%d" % b] for b in blocks]
-    icol = [6 * (b // 3) + b % 3 for b in blocks]
-    NC, FC = PAIR * me, PAIR * (1 - me)
-    A0 = 0 if rising((r - 1) % N) else RUN
-    B0 = RUN - A0
+    def lands(s, kind):
+        u = (3 - (r - s) % N + (kind == "P")) * CH
+        return [job[0] for call in CALLS for job in call
+                if sender[job[0][0]] == s and job[2] < u + CH and u < job[3]]
 
-    def near(a, b):
-        return T.c1[:, win + a:win + b], T.p1[:, win + a:win + b]
+    def chunks(what):
+        if what in ("pair", "other"):
+            p = r // 2 if what == "pair" else 1 - r // 2
+            return [(s, kind) for s in (2 * p, 2 * p + 1) for kind in "RP"]
+        return [(sender[what[-1]], kind) for kind in what[:-1] or "RP"]
 
-    def far(a, b):
+    def side(p, a, b):
+        if p == r // 2:
+            return T.c1[:, win + a:win + b], T.p1[:, win + a:win + b]
         return T.c2[:, a:b], T.p2[:, a:b]
 
-    def product(j, side, u, bank, a, b):
-        st = (near if j < 3 else far)(CH + 128 * (j % 3), CH + 128 * (j % 3) + 128)
-        mv = side(a, b)
-        return tick("t", PE.matmul_mx(PS[u][:, 512 * bank:512 * bank + b - a], st[0], st[1], mv[0], mv[1], True, True))
+    pure = {s: 3 * (s // 2) + 2 * (s % 2) for s in range(N)}
+    mixed = {s: 3 * (s // 2) + 1 for s in range(N)}
+    blocks = [pure[sender[c]] for c in "obn"] + [mixed[sender[c]] for c in "ba"] + [pure[sender["a"]]]
+    W = [T["w%d" % j] for j in range(6)]
+    Y = [T["yb%d" % j] for j in range(6)]
+    Q = {"v": V, "s": S}
 
-    v_ga, s_ga = {}, {}
-    readers = {}
+    readers, arrived, bank = {}, set(), 0
+    out = [{"R": {"v": v_co}, "P": {"v": v_co}} for _ in range(6)]
+    done = [{} for _ in range(6)]
+    PE.wait_ge(sem.v, v_own)
+    for q, what, j in PLAN:
+        if what[:4] in ("mine", "prev"):
+            kind = "R" if what[:4] == "mine" else "P"
+            for k, n in out[j][kind].items():
+                Q[q].wait_ge(sem[k], n)
+            a, b = {"": (0, 32), "0": (0, 16), "1": (16, 32)}[what[4:]]
+            if kind == "P":
+                a, b = a + 32, b + 32
+            w, c = (0, 0) if kind == "R" else (PAIR, 16)
+            done[j][q] = copy(q, Y[j][:, 16 * a:16 * b], W[j][:, w:w + PAIR].indirect(T.co[:, c + a:c + b]))
+            continue
+        part = sorted((column(s, kind), s, kind) for s, kind in chunks(what))
+        p, i = divmod(blocks[j], 3)
+        need = [lands(s, "R") for s in (2 * p, 2 * p + 1) if blocks[j] in (pure[s], mixed[s])]
+        need += [lands(s, kind) for _, s, kind in part]
+        for s in sum(need, []):
+            if s not in arrived:
+                PE.wait_ge(sem[s], landed[s])
+                arrived.add(s)
+        a, b = part[0][0], part[-1][0] + CH
+        banks = -(-(b - a) // BANK)
+        if bank + banks > 8:
+            bank = 0
+        for u in range(bank, bank + banks):
+            if u in readers:
+                PE.wait_ge(sem[readers[u][0]], readers[u][1])
+        o = BANK * bank - a
+        for c in range(a, b, BANK):
+            e = min(b, c + BANK)
+            t = tick("t", PE.matmul_mx(T.ps[:, o + c:o + e], *side(p, CH + 128 * i, CH + 128 * i + 128),
+                                       *side(part[0][1] // 2, c, e), True, True))
+        Q[q].wait_ge(sem.t, t)
+        runs = []
+        for c, s, kind in part:
+            w = CH * s + (PAIR if kind == "P" else 0)
+            if runs and runs[-1][1] + runs[-1][2] == w and runs[-1][3] == kind:
+                runs[-1][2] += CH
+            else:
+                runs.append([c, w, CH, kind])
+        for c, w, n, kind in sorted(runs, key=lambda x: x[3], reverse=True):
+            out[j][kind][q] = copy(q, W[j][:, w:w + n], T.ps[:, o + c:o + c + n])
+        for u in range(bank, bank + banks):
+            readers[u] = (q, cnt[q])
+        bank += banks
 
-    def free(u):
-        for q, n in readers.get(u, ()):
-            PE.wait_ge(sem[q], n)
-
-    def half(j, side, u):
-        free(u)
-        product(j, side, u, 0, 0, 512)
-        return product(j, side, u, 1, 512, PAIR)
-
-    def by_scalar(j, u, bank, w, n, t):
-        S.wait_ge(sem.t, t)
-        return tick("s", S.activation(W[j][:, w:w + n], PS[u][:, 512 * bank:512 * bank + n], COPY))
-
-    def by_vector(j, u, bank, w, n, t):
-        V.wait_ge(sem.t, t)
-        return tick("v", V.tensor_copy(W[j][:, w:w + n], PS[u][:, 512 * bank:512 * bank + n]))
-
-    def columns(j, vn, sn):
-        for q in (V, S):
-            q.wait_ge(sem.v, max(vn, v_co))
-            q.wait_ge(sem.s, sn)
-        s_ga[j] = tick("s", S.activation(Y[j][:, 0:TC], W[j][:, CH:2 * PAIR].indirect(T.co[:, 0:32]), COPY))
-        v_ga[j] = tick("v", V.tensor_copy(Y[j][:, TC:2 * TC], W[j][:, 0:2 * PAIR].indirect(T.co[:, 32:64])))
-
-    PE.wait_ge(sem.v, vq[3])
-    PE.wait_ge(sem.near, n_near)
-    readers[0] = (("s", by_scalar(0, 0, 0, NC, PAIR, half(0, near, 0))),)
-    PE.wait_ge(sem.far1, n_far1)
-    readers[2] = (("v", by_vector(0, 2, 0, FC + A0, RUN, product(0, far, 2, 0, A0, A0 + RUN))),)
-    PE.wait_ge(sem.far3, n_far3)
-    vn = by_vector(0, 3, 0, FC + B0, CH, product(0, far, 3, 0, B0, B0 + CH))
-    sn = by_scalar(0, 3, 1, FC + B0 + CH, CH, product(0, far, 3, 1, B0 + CH, B0 + RUN))
-    readers[3] = (("v", vn), ("s", sn))
-    columns(0, vn, sn)
-    for j in range(1, 6):
-        u = 2 * (1 - j % 2)
-        sn = by_scalar(j, u, 0, NC, PAIR, half(j, near, u))
-        readers[u] = (("s", sn),)
-        vn = by_vector(j, u + 1, 0, FC, PAIR, half(j, far, u + 1))
-        readers[u + 1] = (("v", vn),)
-        columns(j, vn, sn)
-
-    g.wait_ge(sem.isem, 16)
+    g.wait_ge(sem.v, v_idx)
     for j in range(6):
-        g.wait_ge(sem.v, v_ga[j])
-        g.wait_ge(sem.s, s_ga[j])
-        g.indirect_dma_start(T.y[:], IndirectOffsetOnAxis(ap=T.idx[:, icol[j]:icol[j] + 1], axis=0), Y[j][:], None,
+        for k, n in done[j].items():
+            g.wait_ge(sem[k], n)
+        g.indirect_dma_start(T.y[:], IndirectOffsetOnAxis(ap=T.idx[:, blocks[j]:blocks[j] + 1], axis=0), Y[j][:], None,
                              bounds_check=TC - 1, oob_is_err=False).then_inc(sem.scat, 16)
     g.wait_ge(sem.sent, n_sent)
     g.wait_ge(sem.scat, 96)

from concourse.bass import DstId, RemoteDMATransfer, IndirectOffsetOnAxis
from concourse.mybir import dt, AluOpType, ActivationFunctionType

N, CH, TC = 4, 192, 512
RUN = 2 * CH
PAIR = 2 * RUN
CHAIN = 3 * CH
EMPTY = 100000
SHIFT = 96
BANK = 512
PAD = 64
AHEAD = {"o": 0, "a": 1, "n": 2, "b": 3}

SCRATCH = {
    "xs": ("sbuf", [128, 4 * TC], "bfloat16"),
    "h": ("sbuf", [128, 4 * (N * CH + PAD)], "bfloat16"),
    "sl": ("sbuf", [128, 48], "int32"),
    "so": ("sbuf", [128, 48], "uint16"),
    "ml": ("sbuf", [128, 80], "int32"),
    "co": ("sbuf", [128, 80], "uint16"),
    "fo": ("sbuf", [128, 16], "uint16"),
    "sh": ("sbuf", [128, 1], "float32"),
    "num": ("sbuf", [128, TC // 2], "float32"),
    "inv": ("sbuf", [128, SHIFT + PAIR], "float32"),
    "tr": ("sbuf", [128, 6 * 32], "float32"),
    "up": ("sbuf", [128, 6], "float32"),
    "idx": ("sbuf", [128, 6], "int32"),
    "c1": ("sbuf", [128, CHAIN + PAIR], "float8_e4m3fn_x4"),
    "p1": ("sbuf", [128, CHAIN + PAIR], "uint8"),
    "c2": ("sbuf", [128, PAIR], "float8_e4m3fn_x4"),
    "p2": ("sbuf", [128, PAIR], "uint8"),
    "ps": ("psum", [128, 8 * BANK], "float32"),
}
for _k in range(6):
    SCRATCH["w%d" % _k] = ("sbuf", [128, 2 * PAIR], "float32")
    SCRATCH["yb%d" % _k] = ("sbuf", [128, 2 * TC], "float32")

SEMAPHORES = ["lsem", "xsem", "msem", "rsem", "gsem", "numsem", "v", "s", "t", "sent", "scat",
              "a1", "a2", "b1", "n1"]

PIECES = [(0, 64, 128), (64, 384, 576), (384, 576, 320), (576, 768, 0)]
LISTS = (3, 4)
CALLS = [[("b1", "codes", 0, 64)],
         [("b1", "codes", 64, 384)],
         [("n1", "codes", 192, 384)],
         [("b1", "scales", 0, 384)],
         [("a1", "codes", 384, 576), ("n1", "codes", 384, 576)],
         [("n1", "scales", 192, 576)],
         [("a1", "scales", 384, 768)],
         [("a2", "codes", 576, 768)]]
PLAN = ([("s", "o", 0), ("s", "b", 0), ("v", "b", 1), ("s", "o", 1), ("s", "n", 0), ("v", "Ra", 0), ("v", "n", 1),
         ("s", "mine", 0), ("v", "Pa", 0), ("v", "prev0", 0), ("s", "prev1", 0), ("v", "a", 1), ("s", "mine", 1),
         ("v", "prev", 1)]
        + [step for j in range(2, 6)
           for step in (("s", "pair", j), ("v", "other", j), ("s", "mine", j), ("v", "prev", j))])


def rank_program(g, core, T, topo):
    r = T.rank_of(core)
    if r is None:
        return
    sem = T.sem
    COPY = ActivationFunctionType.Copy
    cnt = {"v": 0, "s": 0, "t": 0}

    def tick(q, ins):
        ins.then_inc(sem[q], 1)
        cnt[q] += 1
        return cnt[q]

    V, S, PE = g.vector, g.scalar, g.tensor

    def copy(q, out, in_):
        return tick(q, V.tensor_copy(out, in_) if q == "v" else S.activation(out, in_, COPY))

    def rising(s):
        return s % 2 == 0

    win = CHAIN if rising(r) else 0
    base = 0 if rising(r) else CHAIN
    order = [(r + k) % N for k in (range(N) if rising(r) else reversed(range(N)))]

    def column(s, kind):
        return {"P": 0, "R": CH}[kind] if rising(s) else {"R": RUN, "P": RUN + CH}[kind]

    for q, e in ((g.sync, 0), (S, 1)):
        q.dma_start(T.sl[16 * e:16 * e + 16, :], T.send[:]).then_inc(sem.lsem, 16)
        q.dma_start(T.xs[64 * e:64 * e + 64, :], T.x[64 * e:64 * e + 64, :]).then_inc(sem.xsem, 16)
    for e in range(2):
        rows = slice(16 * e, 16 * e + 16)
        g.sync.dma_start(T.ml[rows, 0:32], T.mine[:]).then_inc(sem.msem, 16)
        g.sync.dma_start(T.ml[rows, 32:48], T.mine[:, 16 * e:16 * e + 16]).then_inc(sem.msem, 16)
    g.sync.dma_start(T.ml[0:16, 48:80], T.prev[:]).then_inc(sem.msem, 16)
    g.dma_start(T.ml[16:32, 48:80], T.prev[:]).then_inc(sem.gsem, 16)
    g.sync.wait_ge(sem.msem, 80)
    g.sync.wait_ge(sem.gsem, 16)
    for a in range(1, 4):
        g.sync.dma_start(T.ml[32 * a:32 * a + 32, :], T.ml[0:32, :]).then_inc(sem.rsem, 16)

    g.iota(T.num[:], [[1, TC // 2]], 0, 0, allow_small_or_imprecise_dtypes=True).then_inc(sem.numsem, 1)
    for k in range(6):
        tick("v", V.memset(T.inv[:, SHIFT + 128 * k:SHIFT + 128 * k + 32], float(EMPTY)))
    for a in range(4):
        tick("v", V.memset(T.sh[32 * a:32 * a + 32, :], float(SHIFT - 32 * a)))
    pad = 0 if rising(r) else PAD
    a = PAIR if rising(r) else 0
    tick("v", V.memset(T.h[:, 4 * a:4 * (a + PAD)], 0.0))
    V.wait_ge(sem.lsem, 32)
    j = 0
    while j < N:
        m = 1
        while j + m < N and order[j + m] == order[j] + m:
            m += 1
        n = tick("v", V.tensor_scalar(T.so[0:32, 12 * j:12 * (j + m)], T.sl[0:32, 12 * order[j]:12 * (order[j] + m)],
                                      0, 4, AluOpType.max, AluOpType.mult))
        j += m
    V.wait_ge(sem.v, n)
    for a in range(1, 4):
        n = copy("v", T.so[32 * a:32 * a + 32, :], T.so[0:32, :])

    add = AluOpType.add
    made = {}

    def invert():
        V.wait_ge(sem.rsem, 48)
        n = tick("v", V.tensor_scalar(T.fo[:], T.ml[:, 32:48], T.sh[:], None, add))
        made["co"] = copy("v", T.co[:], T.ml[:])
        V.wait_ge(sem.numsem, 1)
        V.wait_ge(sem.v, n)
        made["inv"] = copy("v", T.inv[:].indirect(T.fo[:]), T.num[:])

    def turn():
        V.wait_ge(sem.v, made["inv"])
        for k in range(6):
            a = SHIFT + 128 * k
            n = tick("v", V.transpose(T.tr[:, 32 * k:32 * k + 32], T.inv[:, a:a + 32]))
        V.wait_ge(sem.v, n)
        n = tick("v", V.tensor_scalar(T.up[:], T.tr[:, 16:192:32], TC // 2, None, add))
        V.wait_ge(sem.v, n)
        made["idx"] = tick("v", V.tensor_tensor(T.idx[:], T.tr[:, 0:192:32], T.up[:], AluOpType.min))

    def gathered(t, a, b):
        return T.h[:, 4 * (pad + a) + t:4 * (pad + b):4], T.xs[:, t:4 * TC].indirect(T.so[:, a // 16:b // 16])

    def quantise(a, c0, c1):
        n = c1 - c0
        return tick("v", V.quantize_mx(T.c1[:, a:a + n], T.p1[:, a:a + n], T.h[:, 4 * (pad + c0):4 * (pad + c1)]))

    def span(u0, u1):
        return (PAIR - u1, PAIR - u0) if rising(r) else (u0, u1)

    for q in (V, S):
        q.wait_ge(sem.v, n)
        q.wait_ge(sem.xsem, 32)
    vq = []
    for i, (u0, u1, share) in enumerate(PIECES):
        c0, c1 = span(u0, u1)
        if i == LISTS[0]:
            invert()
        if i == LISTS[1]:
            turn()
        for t in range(4):
            c = c0 + min(max(share - t * (c1 - c0), 0), c1 - c0)
            if c > c0:
                copy("v", *gathered(t, c0, c))
            if c < c1:
                copy("s", *gathered(t, c, c1))
        if share:
            V.wait_ge(sem.v, cnt["v"])
        V.wait_ge(sem.s, cnt["s"])
        c0, c1 = span(min(u0, u1 - 128), u1)
        vq.append((u0, u1, quantise(base + c0, c0, c1)))
    v_own = quantise(win + column(r, "R"), *span(CHAIN, PAIR))
    if LISTS[0] == len(PIECES):
        invert()
    if LISTS[1] == len(PIECES):
        turn()
    v_co, v_idx = made["co"], made["idx"]

    dsts = {k: T.cores[(r + k) % N] for k in (1, 2, 3)}
    feng = topo.engines(core, dsts[1])
    neng = [e for e in topo.engines(core, dsts[2]) if e not in feng]
    landed = {}

    def transfer(lands, what, u0, u1):
        k = AHEAD[lands[0]]
        d = (r + k) % N
        rid, pid, _ = topo.addr(dsts[k])
        same = r // 2 == d // 2
        c0, c1 = span(u0, u1)
        run = span((3 - k) * CH, (5 - k) * CH)[0]
        c = ((CHAIN if rising(d) else 0) if same else 0) + (0 if rising(r) else RUN) + c0 - run
        a, n = base + c0, c1 - c0
        if what == "scales":
            i, o = T.p1[:, a:a + n], (T.p1 if same else T.p2)[:, c:c + n]
        else:
            i, o = T.c1[:, a:a + n].bitcast(dt.uint8), (T.c1 if same else T.c2)[:, c:c + n].bitcast(dt.uint8)
        es = neng if k == 2 else feng
        landed[lands] = landed.get(lands, 0) + len(es)
        return RemoteDMATransfer(dst_ids=[DstId(rid=rid, pnc=pid)], remote_sem=sem[lands], src=i, dst=o,
                                 dma_engine_mask=sum(1 << e for e in es))

    seen = 0
    for call in CALLS:
        n = max(n for u0, u1, n in vq for job in call if u0 < job[3] and job[2] < u1)
        if n > seen:
            g.wait_ge(sem.v, n)
            seen = n
        g.remote_dma_fused([transfer(*job) for job in call], local_sem=sem.sent)
    n_sent = sum(landed.values())

    sender = {c: (r - k) % N for c, k in AHEAD.items()}

    def lands(s, kind):
        u = (3 - (r - s) % N + (kind == "P")) * CH
        return [job[0] for call in CALLS for job in call
                if sender[job[0][0]] == s and job[2] < u + CH and u < job[3]]

    def chunks(what):
        if what in ("pair", "other"):
            p = r // 2 if what == "pair" else 1 - r // 2
            return [(s, kind) for s in (2 * p, 2 * p + 1) for kind in "RP"]
        return [(sender[what[-1]], kind) for kind in what[:-1] or "RP"]

    def side(p, a, b):
        if p == r // 2:
            return T.c1[:, win + a:win + b], T.p1[:, win + a:win + b]
        return T.c2[:, a:b], T.p2[:, a:b]

    pure = {s: 3 * (s // 2) + 2 * (s % 2) for s in range(N)}
    mixed = {s: 3 * (s // 2) + 1 for s in range(N)}
    blocks = [pure[sender[c]] for c in "obn"] + [mixed[sender[c]] for c in "ba"] + [pure[sender["a"]]]
    W = [T["w%d" % j] for j in range(6)]
    Y = [T["yb%d" % j] for j in range(6)]
    Q = {"v": V, "s": S}

    readers, arrived, bank = {}, set(), 0
    out = [{"R": {"v": v_co}, "P": {"v": v_co}} for _ in range(6)]
    done = [{} for _ in range(6)]
    PE.wait_ge(sem.v, v_own)
    for q, what, j in PLAN:
        if what[:4] in ("mine", "prev"):
            kind = "R" if what[:4] == "mine" else "P"
            for k, n in out[j][kind].items():
                Q[q].wait_ge(sem[k], n)
            a, b = {"": (0, 32), "0": (0, 16), "1": (16, 32)}[what[4:]]
            if kind == "P":
                a, b = a + 32, b + 32
            w, c = (0, 0) if kind == "R" else (PAIR, 16)
            done[j][q] = copy(q, Y[j][:, 16 * a:16 * b], W[j][:, w:w + PAIR].indirect(T.co[:, c + a:c + b]))
            continue
        part = sorted((column(s, kind), s, kind) for s, kind in chunks(what))
        p, i = divmod(blocks[j], 3)
        need = [lands(s, "R") for s in (2 * p, 2 * p + 1) if blocks[j] in (pure[s], mixed[s])]
        need += [lands(s, kind) for _, s, kind in part]
        for s in sum(need, []):
            if s not in arrived:
                PE.wait_ge(sem[s], landed[s])
                arrived.add(s)
        a, b = part[0][0], part[-1][0] + CH
        banks = -(-(b - a) // BANK)
        if bank + banks > 8:
            bank = 0
        for u in range(bank, bank + banks):
            if u in readers:
                PE.wait_ge(sem[readers[u][0]], readers[u][1])
        o = BANK * bank - a
        for c in range(a, b, BANK):
            e = min(b, c + BANK)
            t = tick("t", PE.matmul_mx(T.ps[:, o + c:o + e], *side(p, CH + 128 * i, CH + 128 * i + 128),
                                       *side(part[0][1] // 2, c, e), True, True))
        Q[q].wait_ge(sem.t, t)
        runs = []
        for c, s, kind in part:
            w = CH * s + (PAIR if kind == "P" else 0)
            if runs and runs[-1][1] + runs[-1][2] == w and runs[-1][3] == kind:
                runs[-1][2] += CH
            else:
                runs.append([c, w, CH, kind])
        for c, w, n, kind in sorted(runs, key=lambda x: x[3], reverse=True):
            out[j][kind][q] = copy(q, W[j][:, w:w + n], T.ps[:, o + c:o + c + n])
        for u in range(bank, bank + banks):
            readers[u] = (q, cnt[q])
        bank += banks

    g.wait_ge(sem.v, v_idx)
    for j in range(6):
        for k, n in done[j].items():
            g.wait_ge(sem[k], n)
        g.indirect_dma_start(T.y[:], IndirectOffsetOnAxis(ap=T.idx[:, blocks[j]:blocks[j] + 1], axis=0), Y[j][:], None,
                             bounds_check=TC - 1, oob_is_err=False).then_inc(sem.scat, 16)
    g.wait_ge(sem.sent, n_sent)
    g.wait_ge(sem.scat, 96)
